import numpy as np
CORES = [0,8]
N = 2
def setup_inputs(rng):
    return {"x": rng.standard_normal((N, 128, 16384), dtype=np.float32)}
def reference(x):
    s = x.sum(axis=0, dtype=np.float64).astype(x.dtype)
    return {"y": np.broadcast_to(s, (N,) + s.shape)}

@@ -1,0 +1,69 @@
+import concourse.bass as bass
+
+NCH = 16
+W = 16384 // NCH
+HELP = (2, 3, 6, 7)
+PRE = 2
+LAG = 1
+
+SCRATCH = {
+    "xs": ("sbuf", [128, 16384], "float32"),
+    "land": ("sbuf", [128, 16384], "float32"),
+}
+SEMAPHORES = ["ld0", "ld1", "st", "snt"] + ["a%d" % i for i in range(16)] + ["b%d" % i for i in range(4)]
+
+
+def rank_program(g, core, T, topo):
+    A = [T.sem.a0, T.sem.a1, T.sem.a2, T.sem.a3, T.sem.a4, T.sem.a5, T.sem.a6, T.sem.a7,
+         T.sem.a8, T.sem.a9, T.sem.a10, T.sem.a11, T.sem.a12, T.sem.a13, T.sem.a14, T.sem.a15]
+    B = [T.sem.b0, T.sem.b1, T.sem.b2, T.sem.b3]
+    LD = [T.sem.ld0, T.sem.ld1]
+    base = topo.chip(core) * 8
+    root = base
+    on_chip = core - base
+
+    def blk(t, k):
+        return t[:, k * W:(k + 1) * W]
+
+    if core == root:
+        def load(k):
+            g.dma_start(blk(T.xs, k), blk(T.x, k)).then_inc(LD[k % PRE], 16)
+
+        for k in range(min(PRE, NCH)):
+            load(k)
+        for k in range(NCH):
+            g.wait_ge(LD[k % PRE], 16 * (k // PRE + 1))
+            rid, pid = topo.addr(base + HELP[k % 4])[:2]
+            g.remote_dma(blk(T.xs, k), blk(T.xs, k), A[k], T.sem.snt, pid, rid, 0xFFFF)
+            if k + PRE < NCH:
+                load(k + PRE)
+        for k in range(NCH):
+            g.wait_ge(A[k], 8)
+            g.dma_start(blk(T.y, k), blk(T.land, k)).then_inc(T.sem.st, 16)
+        g.wait_ge(T.sem.snt, 16 * NCH)
+        g.wait_ge(T.sem.st, 16 * NCH)
+        return
+
+    if on_chip not in HELP:
+        return
+
+    mate_rid, mate_pid = topo.addr(core ^ 8)[:2]
+    root_rid, root_pid = topo.addr(root)[:2]
+    mine = [k for k in range(NCH) if HELP[k % 4] == on_chip]
+
+    def fold(k):
+        g.wait_ge(B[k // 4], 8)
+        g.remote_dma_fused(
+            [bass.RemoteDMATransfer(dst_ids=[bass.DstId(rid=root_rid, pnc=root_pid)], dma_engine_mask=0xFF00,
+                                    remote_sem=A[k], srcs=[blk(T.xs, k), blk(T.land, k)],
+                                    dsts=[blk(T.land, k)], alu_op=1)],
+            local_sem=T.sem.snt)
+
+    for i, k in enumerate(mine):
+        g.wait_ge(A[k], 16)
+        g.remote_dma(blk(T.land, k), blk(T.xs, k), B[k // 4], T.sem.snt, mate_pid, mate_rid, 0x00FF)
+        if i >= LAG:
+            fold(mine[i - LAG])
+    for k in mine[len(mine) - LAG:]:
+        fold(k)
+    g.wait_ge(T.sem.snt, 16 * len(mine))

@@ -1,7 +1,8 @@
 import concourse.bass as bass
 
-NCH = 16
-W = 16384 // NCH
+WIDTHS = [128, 384, 512, 512, 512, 512, 512, 512, 384, 128]
+NR = len(WIDTHS)
+STARTS = [4 * sum(WIDTHS[:r]) for r in range(NR)]
 HELP = (2, 3, 6, 7)
 PRE = 2
 LAG = 1
@@ -10,60 +11,71 @@ SCRATCH = {
     "xs": ("sbuf", [128, 16384], "float32"),
     "land": ("sbuf", [128, 16384], "float32"),
 }
-SEMAPHORES = ["ld0", "ld1", "st", "snt"] + ["a%d" % i for i in range(16)] + ["b%d" % i for i in range(4)]
+SEMAPHORES = (["ld0", "ld1", "ld2", "ld3", "st", "snt"] + ["a%d" % i for i in range(16)]
+              + ["b%d" % i for i in range(16)])
 
 
 def rank_program(g, core, T, topo):
     A = [T.sem.a0, T.sem.a1, T.sem.a2, T.sem.a3, T.sem.a4, T.sem.a5, T.sem.a6, T.sem.a7,
          T.sem.a8, T.sem.a9, T.sem.a10, T.sem.a11, T.sem.a12, T.sem.a13, T.sem.a14, T.sem.a15]
-    B = [T.sem.b0, T.sem.b1, T.sem.b2, T.sem.b3]
-    LD = [T.sem.ld0, T.sem.ld1]
+    B = [T.sem.b0, T.sem.b1, T.sem.b2, T.sem.b3, T.sem.b4, T.sem.b5, T.sem.b6, T.sem.b7,
+         T.sem.b8, T.sem.b9, T.sem.b10, T.sem.b11, T.sem.b12, T.sem.b13, T.sem.b14, T.sem.b15]
+    LD = [T.sem.ld0, T.sem.ld1, T.sem.ld2, T.sem.ld3]
     base = topo.chip(core) * 8
     root = base
     on_chip = core - base
 
-    def blk(t, k):
-        return t[:, k * W:(k + 1) * W]
+    def rnd(t, r):
+        return t[:, STARTS[r]:STARTS[r] + 4 * WIDTHS[r]]
+
+    def blk(t, r, h):
+        c = STARTS[r] + h * WIDTHS[r]
+        return t[:, c:c + WIDTHS[r]]
 
     if core == root:
-        def load(k):
-            g.dma_start(blk(T.xs, k), blk(T.x, k)).then_inc(LD[k % PRE], 16)
+        def load(r):
+            g.dma_start(rnd(T.xs, r), rnd(T.x, r)).then_inc(LD[r % PRE], 16)
 
-        for k in range(min(PRE, NCH)):
-            load(k)
-        for k in range(NCH):
-            g.wait_ge(LD[k % PRE], 16 * (k // PRE + 1))
-            rid, pid = topo.addr(base + HELP[k % 4])[:2]
-            g.remote_dma(blk(T.xs, k), blk(T.xs, k), A[k], T.sem.snt, pid, rid, 0xFFFF)
-            if k + PRE < NCH:
-                load(k + PRE)
-        for k in range(NCH):
-            g.wait_ge(A[k], 8)
-            g.dma_start(blk(T.y, k), blk(T.land, k)).then_inc(T.sem.st, 16)
-        g.wait_ge(T.sem.snt, 16 * NCH)
-        g.wait_ge(T.sem.st, 16 * NCH)
+        for r in range(min(PRE, NR)):
+            load(r)
+        for r in range(NR):
+            g.wait_ge(LD[r % PRE], 16 * (r // PRE + 1))
+            trs = []
+            for h in range(4):
+                rid, pid = topo.addr(base + HELP[h])[:2]
+                trs.append(bass.RemoteDMATransfer(dst_ids=[bass.DstId(rid=rid, pnc=pid)],
+                                                  dma_engine_mask=0xF << (4 * h), remote_sem=A[r],
+                                                  src=blk(T.xs, r, h), dst=blk(T.xs, r, h)))
+            g.remote_dma_fused(trs, local_sem=T.sem.snt)
+            if r + PRE < NR:
+                load(r + PRE)
+        for r in range(NR):
+            g.wait_ge(A[r], 32)
+            g.dma_start(rnd(T.y, r), rnd(T.land, r)).then_inc(T.sem.st, 16)
+        g.wait_ge(T.sem.snt, 16 * NR)
+        g.wait_ge(T.sem.st, 16 * NR)
         return
 
     if on_chip not in HELP:
         return
 
+    h = HELP.index(on_chip)
     mate_rid, mate_pid = topo.addr(core ^ 8)[:2]
     root_rid, root_pid = topo.addr(root)[:2]
-    mine = [k for k in range(NCH) if HELP[k % 4] == on_chip]
 
-    def fold(k):
-        g.wait_ge(B[k // 4], 8)
+    def fold(r):
+        g.wait_ge(B[r], 8)
         g.remote_dma_fused(
             [bass.RemoteDMATransfer(dst_ids=[bass.DstId(rid=root_rid, pnc=root_pid)], dma_engine_mask=0xFF00,
-                                    remote_sem=A[k], srcs=[blk(T.xs, k), blk(T.land, k)],
-                                    dsts=[blk(T.land, k)], alu_op=1)],
+                                    remote_sem=A[r], srcs=[blk(T.xs, r, h), blk(T.land, r, h)],
+                                    dsts=[blk(T.land, r, h)], alu_op=1)],
             local_sem=T.sem.snt)
 
-    for i, k in enumerate(mine):
-        g.wait_ge(A[k], 16)
-        g.remote_dma(blk(T.land, k), blk(T.xs, k), B[k // 4], T.sem.snt, mate_pid, mate_rid, 0x00FF)
-        if i >= LAG:
-            fold(mine[i - LAG])
-    for k in mine[len(mine) - LAG:]:
-        fold(k)
-    g.wait_ge(T.sem.snt, 16 * len(mine))
+    for r in range(NR):
+        g.wait_ge(A[r], 4)
+        g.remote_dma(blk(T.land, r, h), blk(T.xs, r, h), B[r], T.sem.snt, mate_pid, mate_rid, 0x00FF)
+        if r >= LAG:
+            fold(r - LAG)
+    for r in range(NR - LAG, NR):
+        fold(r)
+    g.wait_ge(T.sem.snt, 16 * NR)

@@ -11,7 +11,7 @@ SCRATCH = {
     "xs": ("sbuf", [128, 16384], "float32"),
     "land": ("sbuf", [128, 16384], "float32"),
 }
-SEMAPHORES = (["ld0", "ld1", "ld2", "ld3", "st", "snt"] + ["a%d" % i for i in range(16)]
+SEMAPHORES = (["ld0", "ld1", "st", "snt"] + ["a%d" % i for i in range(16)]
               + ["b%d" % i for i in range(16)])
 
 
@@ -20,7 +20,7 @@ def rank_program(g, core, T, topo):
          T.sem.a8, T.sem.a9, T.sem.a10, T.sem.a11, T.sem.a12, T.sem.a13, T.sem.a14, T.sem.a15]
     B = [T.sem.b0, T.sem.b1, T.sem.b2, T.sem.b3, T.sem.b4, T.sem.b5, T.sem.b6, T.sem.b7,
          T.sem.b8, T.sem.b9, T.sem.b10, T.sem.b11, T.sem.b12, T.sem.b13, T.sem.b14, T.sem.b15]
-    LD = [T.sem.ld0, T.sem.ld1, T.sem.ld2, T.sem.ld3]
+    LD = [T.sem.ld0, T.sem.ld1]
     base = topo.chip(core) * 8
     root = base
     on_chip = core - base

import concourse.bass as bass

WIDTHS = [128, 384, 512, 512, 512, 512, 512, 512, 384, 128]
NR = len(WIDTHS)
STARTS = [4 * sum(WIDTHS[:r]) for r in range(NR)]
HELP = (2, 3, 6, 7)
PRE = 2
LAG = 1

SCRATCH = {
    "xs": ("sbuf", [128, 16384], "float32"),
    "land": ("sbuf", [128, 16384], "float32"),
}
SEMAPHORES = (["ld0", "ld1", "st", "snt"] + ["a%d" % i for i in range(16)]
              + ["b%d" % i for i in range(16)])


def rank_program(g, core, T, topo):
    A = [T.sem.a0, T.sem.a1, T.sem.a2, T.sem.a3, T.sem.a4, T.sem.a5, T.sem.a6, T.sem.a7,
         T.sem.a8, T.sem.a9, T.sem.a10, T.sem.a11, T.sem.a12, T.sem.a13, T.sem.a14, T.sem.a15]
    B = [T.sem.b0, T.sem.b1, T.sem.b2, T.sem.b3, T.sem.b4, T.sem.b5, T.sem.b6, T.sem.b7,
         T.sem.b8, T.sem.b9, T.sem.b10, T.sem.b11, T.sem.b12, T.sem.b13, T.sem.b14, T.sem.b15]
    LD = [T.sem.ld0, T.sem.ld1]
    base = topo.chip(core) * 8
    root = base
    on_chip = core - base

    def rnd(t, r):
        return t[:, STARTS[r]:STARTS[r] + 4 * WIDTHS[r]]

    def blk(t, r, h):
        c = STARTS[r] + h * WIDTHS[r]
        return t[:, c:c + WIDTHS[r]]

    if core == root:
        def load(r):
            g.dma_start(rnd(T.xs, r), rnd(T.x, r)).then_inc(LD[r % PRE], 16)

        for r in range(min(PRE, NR)):
            load(r)
        for r in range(NR):
            g.wait_ge(LD[r % PRE], 16 * (r // PRE + 1))
            trs = []
            for h in range(4):
                rid, pid = topo.addr(base + HELP[h])[:2]
                trs.append(bass.RemoteDMATransfer(dst_ids=[bass.DstId(rid=rid, pnc=pid)],
                                                  dma_engine_mask=0xF << (4 * h), remote_sem=A[r],
                                                  src=blk(T.xs, r, h), dst=blk(T.xs, r, h)))
            g.remote_dma_fused(trs, local_sem=T.sem.snt)
            if r + PRE < NR:
                load(r + PRE)
        for r in range(NR):
            g.wait_ge(A[r], 32)
            g.dma_start(rnd(T.y, r), rnd(T.land, r)).then_inc(T.sem.st, 16)
        g.wait_ge(T.sem.snt, 16 * NR)
        g.wait_ge(T.sem.st, 16 * NR)
        return

    if on_chip not in HELP:
        return

    h = HELP.index(on_chip)
    mate_rid, mate_pid = topo.addr(core ^ 8)[:2]
    root_rid, root_pid = topo.addr(root)[:2]

    def fold(r):
        g.wait_ge(B[r], 8)
        g.remote_dma_fused(
            [bass.RemoteDMATransfer(dst_ids=[bass.DstId(rid=root_rid, pnc=root_pid)], dma_engine_mask=0xFF00,
                                    remote_sem=A[r], srcs=[blk(T.xs, r, h), blk(T.land, r, h)],
                                    dsts=[blk(T.land, r, h)], alu_op=1)],
            local_sem=T.sem.snt)

    for r in range(NR):
        g.wait_ge(A[r], 4)
        g.remote_dma(blk(T.land, r, h), blk(T.xs, r, h), B[r], T.sem.snt, mate_pid, mate_rid, 0x00FF)
        if r >= LAG:
            fold(r - LAG)
    for r in range(NR - LAG, NR):
        fold(r)
    g.wait_ge(T.sem.snt, 16 * NR)
